import numpy as np
import ml_dtypes


def mxq(x, axis, fmt="e4m3"):
    dtype, down = {"e4m3": (ml_dtypes.float8_e4m3fn, 7), "e5m2": (ml_dtypes.float8_e5m2, 14)}[fmt]
    v = np.moveaxis(np.asarray(x, np.float32).astype(ml_dtypes.bfloat16).astype(np.float64), axis, -1)
    blocks = v.reshape(v.shape[:-1] + (-1, 32))
    amax = np.abs(blocks).max(-1, keepdims=True)
    byte = np.maximum(np.where(amax > 0, np.frexp(amax)[1] - 1 + 127, 0) - down, 1)
    scale = np.exp2(byte - 127.0)
    codes = (blocks / scale).astype(np.float32).astype(dtype).astype(np.float64)
    return np.moveaxis((codes * scale).reshape(v.shape), -1, axis)


WIDE = False


def mx_kscale(k):
    if not WIDE:
        return np.ones(k)
    levels = np.array([10, -10, 5, -5, 0])
    if k % 512:
        return np.exp2(np.random.permutation(np.resize(levels, k // 32))).repeat(32)
    a = np.empty((k // 512, 16))
    for p in range(k // 512):
        a[p, :8] = np.random.permutation(np.resize(levels, 8))
        for g in range(8):
            far = levels[np.abs(levels - a[p, g]) >= 10]
            a[p, g + 8] = far[np.random.randint(len(far))]
    return np.exp2(a.ravel()).repeat(32)


def f64(x):
    return np.asarray(x).astype(np.float64)


def striped(idx):
    return np.tile(idx.reshape(-1, 16).T, (8, 1)).astype(np.uint16)


def unstriped(offs):
    return offs[:16].T.reshape(-1).astype(np.int64)


def striped8(idx):
    return np.concatenate([x.reshape(-1, 16).T for x in idx]).astype(np.uint16)


def runs(offs, k):
    lists = np.stack([offs[16 * r : 16 * r + 16].T.reshape(-1) for r in range(8)]).astype(np.int64)
    return lists[np.arange(k) % 512 // 64]


def pack_weight(w):
    k, n = w.shape
    w = f64(np.asarray(w, np.float32).astype(ml_dtypes.bfloat16)).reshape(k // 32, 32, n)
    amax = np.abs(w).max(1)
    byte = np.clip(np.where(amax > 0, np.frexp(amax)[1] - 1 + 127 - 7, 1), 1, 254)
    scaled = (w * np.exp2(127.0 - byte)[:, None, :]).reshape(k, n).astype(np.float32)
    words = np.ascontiguousarray(scaled.reshape(k // 512, 128, 4, n).transpose(0, 1, 3, 2)).astype(ml_dtypes.float8_e4m3fn).view(np.uint8)
    return words, np.ascontiguousarray(byte.astype(np.uint8).reshape(k // 512, 16, n))


def unpack_weight(words, scales):
    g, p, n, _ = words.shape
    vals = np.ascontiguousarray(words).view(ml_dtypes.float8_e4m3fn).astype(np.float64) * np.repeat(np.exp2(scales.astype(np.float64) - 127.0), 8, axis=1)[..., None]
    return vals.transpose(0, 1, 3, 2).reshape(g * 512, n)


K, T, S, H, C = 512, 2048, 512, 512, 512


def setup_inputs():
    n = np.random.standard_normal
    s = mx_kscale(K)[:, None]
    packed_xT = pack_weight(n((K, T)) * s)
    return {
        "x_words": packed_xT[0],
        "x_scales": packed_xT[1],
        "w1": (n((K, H)) / np.sqrt(K) / s).astype(np.float32),
        "gs": (np.random.uniform(0.5, 1.5, (K, 1)) / s).astype(np.float32),
        "offs": striped(np.random.permutation(T)[:S]),
        "n1": striped8(np.stack([np.random.permutation(S) for _ in range(8)])),
        "n2": striped8(np.stack([np.random.permutation(S) for _ in range(8)])),
        "ca": striped(np.random.permutation(T)[:C]),
        "cb": striped(np.random.permutation(T)[:C]),
        "cd": striped(np.random.permutation(T)[:C]),
        "n3": striped8(np.stack([np.random.permutation(S) for _ in range(8)])),
        "n4": striped8(np.stack([np.random.permutation(S) for _ in range(8)])),
        "n5": striped(np.random.permutation(S)),
        "n6": striped(np.random.permutation(S)),
    }


def reference(x_words, x_scales, w1, gs, offs, n1, n2, ca, cb, cd, n3, n4, n5, n6):
    x_ca = unpack_weight(x_words, x_scales)[:, unstriped(ca)]
    xq = unpack_weight(x_words, x_scales)[:, unstriped(offs)]
    y = mxq(f64(w1), 0, "e4m3").T @ xq
    st = y + 0.5 * (y[np.arange(H)[:, None], runs(n1, H)])
    z = f64(gs) * (st - (st[np.arange(H)[:, None], runs(n2, H)]))
    zq = mxq(z, 0, "e4m3")
    a = 0.0625 * (x_ca.T @ zq)
    x_cb = unpack_weight(x_words, x_scales)[:, unstriped(cb)]
    b = 0.0625 * (x_cb.T @ zq)
    m1 = np.maximum(a, b[np.arange(C)[:, None], runs(n4, C)]) - (np.minimum(a[np.arange(C)[:, None], runs(n3, C)], b))
    x_cd = unpack_weight(x_words, x_scales)[:, unstriped(cd)]
    q = 0.0625 * (x_cd.T @ zq)
    return (m1 - m1[:, unstriped(n5)]) / (np.abs(q) + np.abs(q[:, unstriped(n6)]) + 0.5)

@@ -1,0 +1,201 @@
+from contextlib import ExitStack
+
+import concourse.mybir as mybir
+
+F32 = mybir.dt.float32
+BF16 = mybir.dt.bfloat16
+I32 = mybir.dt.int32
+U32 = mybir.dt.uint32
+U16 = mybir.dt.uint16
+U8 = mybir.dt.uint8
+FP8X4 = mybir.dt.float8_e4m3fn_x4
+ALU = mybir.AluOpType
+ACT = mybir.ActivationFunctionType
+
+P = 128
+T = 2048
+S = 512
+NT = 4
+HALF = S // 2
+LCOLS = S // 16
+
+FLOPS = 4 * 2 * 512 * 512 * 512
+
+
+def tile_picked_tricdmaxbnormbhop_none_p_kernel(
+    tc, x_words, x_scales, w1, gs, offs, n1, n2, ca, cb, cd, n3, n4, n5, n6, out
+):
+    nc = tc.nc
+    with ExitStack() as ctx:
+        keep = ctx.enter_context(tc.tile_pool(name="keep", bufs=1))
+        psum = ctx.enter_context(tc.psum_pool(name="psum", bufs=1))
+
+        def load_list(name, ap):
+            tl = keep.tile([P, LCOLS], U16, name="list_" + name)
+            nc.sync.dma_start(tl[:], ap)
+            return tl
+
+        def four(name, width):
+            return [keep.tile([P, width], F32, name="%s%d" % (name, t)) for t in range(NT)]
+
+        xs = keep.tile([P, T], U8, name="xs")
+        nc.gpsimd.memset(xs[:].bitcast(I32), 0)
+        l_offs = load_list("offs", offs)
+        for qd in range(4):
+            nc.scalar.dma_start(
+                xs[32 * qd : 32 * qd + 4, :].bitcast(I32),
+                x_scales[0, 4 * qd : 4 * qd + 4, :].bitcast(I32),
+            )
+        l_cd = load_list("cd", cd)
+        w_raw = keep.tile([P, 4, S], F32, name="w_raw")
+        nc.sync.dma_start(w_raw[:], w1.rearrange("(p j) c -> p j c", j=4))
+        xw = keep.tile([P, T], I32, name="xw")
+        nc.sync.dma_start(xw[:], x_words[0].rearrange("p n t -> p (n t)").bitcast(I32))
+        gs_t = keep.tile([P, NT], F32, name="gs_t")
+        nc.gpsimd.dma_start(gs_t[:], gs.rearrange("(p t) o -> p (t o)", t=NT))
+        l_n1 = load_list("n1", n1)
+        l_ca = load_list("ca", ca)
+        l_n2 = load_list("n2", n2)
+        l_cb = load_list("cb", cb)
+        l_n6 = load_list("n6", n6)
+        l_n4 = load_list("n4", n4)
+        l_n3 = load_list("n3", n3)
+        l_n5 = load_list("n5", n5)
+
+        yq = four("yq", 2 * S)
+        for t in range(NT):
+            nc.gpsimd.memset(yq[t][:, S:], 0.0)
+        eight = keep.tile([P, 1], F32, name="eight")
+        nc.gpsimd.memset(eight[:], 8.0)
+        gs_half = keep.tile([P, NT], F32, name="gs_half")
+        nc.gpsimd.tensor_scalar(gs_half[:], gs_t[:], 0.5, 0.0, ALU.mult, ALU.add)
+
+        def gather_bytes(name, lst, dealt, tag):
+            got = keep.tile([P, S], U8, name="bytes_" + name, tag=tag, align_bytes=64)
+            nc.vector.tensor_copy(got[:], xs[:].indirect(lst[:]))
+            if not dealt:
+                return got
+            res = keep.tile([P, S], U8, name="dealt_" + name, align_bytes=64)
+            nc.vector.tensor_copy(
+                res[:].bitcast(I32).rearrange("p (t u) -> p t u", t=NT),
+                got[:].bitcast(I32).rearrange("p (u t) -> p t u", t=NT),
+            )
+            return res
+
+        def gather_words(name, lst, dealt, tag):
+            got = keep.tile([P, S], U32, name="words_" + name, tag=tag, align_bytes=64)
+            view = got[:].rearrange("p (t u b) -> p u t b", t=NT, b=4) if dealt else got[:]
+            nc.vector.tensor_copy(view, xw[:].bitcast(U32).indirect(lst[:]))
+            return got
+
+        xq_s = gather_bytes("offs", l_offs, False, "xq_s")
+        cd_s = gather_bytes("cd", l_cd, True, "cd_s")
+
+        w_bf = keep.tile([P, NT * P * 4], BF16, name="w_bf", tag="w_bf", align_bytes=64)
+        nc.scalar.activation(
+            w_bf[:].rearrange("p (t m j) -> p m t j", t=NT, j=4),
+            w_raw[:].rearrange("p j (m t) -> p m t j", t=NT),
+            ACT.Copy,
+        )
+        xq_w = gather_words("offs", l_offs, False, "xq_w")
+        w_codes = keep.tile([P, S], U32, name="w_codes", tag="w_codes", align_bytes=64)
+        w_scales = keep.tile([P, S], U8, name="w_scales", tag="w_scales", align_bytes=64)
+        nc.vector.quantize_mx(out=w_codes[:].bitcast(FP8X4), scales=w_scales[:], in_=w_bf[:])
+
+        def bank(i):
+            return psum.tile([P, S], F32, name="bank%d" % i)
+
+        def mm(dst, words, scales, t, rw, rs):
+            cols = slice(t * P, (t + 1) * P)
+            nc.tensor.matmul_mx(
+                out=dst, lhsT=words[:, cols].bitcast(FP8X4), lhsT_scale=scales[:, cols],
+                rhs=rw.bitcast(FP8X4), rhs_scale=rs, start=True, stop=True,
+            )
+
+        sa = four("sa", 2 * S)
+        for t in range(NT):
+            y_ps = bank(t)
+            mm(y_ps[:], w_codes, w_scales, t, xq_w[:], xq_s[:])
+            nc.scalar.activation(yq[t][:, :S], y_ps[:], ACT.Copy, scale=gs_half[:, t : t + 1])
+            nc.scalar.activation(sa[t][:, S:], yq[t][:].indirect(l_n1[:]), ACT.Copy)
+            nc.vector.scalar_tensor_tensor(
+                sa[t][:, :S], y_ps[:], gs_t[:, t : t + 1], sa[t][:, S:], ALU.mult, ALU.add
+            )
+
+        cd_w = gather_words("cd", l_cd, True, "w_bf")
+        ca_w = gather_words("ca", l_ca, True, "w_codes")
+        ca_s = gather_bytes("ca", l_ca, True, "w_scales")
+
+        bg = four("bg", 2 * S)
+        z_codes = keep.tile([P, S], U32, name="z_codes", align_bytes=64)
+        z_scales = keep.tile([P, S], U8, name="z_scales", align_bytes=64)
+        q_ps = [bank(NT + t) for t in range(NT)]
+        a_ps = [bank(t) for t in range(NT)]
+        for h in range(2):
+            for t in range(NT):
+                nc.scalar.activation(
+                    bg[t][:, S + h * HALF : S + (h + 1) * HALF],
+                    sa[t][:].indirect(l_n2[:, h * LCOLS // 2 : (h + 1) * LCOLS // 2]),
+                    ACT.Copy,
+                )
+        for h in range(2):
+            cols = slice(h * HALF, (h + 1) * HALF)
+            planes = keep.tile([P, NT, HALF], BF16, name="planes%d" % h, tag="planes%d" % h, align_bytes=64)
+            for t in range(NT):
+                nc.vector.tensor_tensor(
+                    planes[:, t, :], sa[t][:, cols], bg[t][:, S + h * HALF : S + (h + 1) * HALF], ALU.subtract
+                )
+            z_bf = keep.tile([P, HALF * 4], BF16, name="z_bf%d" % h, tag="z_bf%d" % h, align_bytes=64)
+            nc.vector.tensor_copy(
+                z_bf[:].rearrange("p (c i t) -> p c t i", i=4, t=NT),
+                planes[:].rearrange("p t (c i) -> p c t i", i=4),
+            )
+            nc.vector.quantize_mx(out=z_codes[:, cols].bitcast(FP8X4), scales=z_scales[:, cols], in_=z_bf[:])
+            for t in range(NT):
+                mm(q_ps[t][:, cols], cd_w, cd_s, t, z_codes[:, cols], z_scales[:, cols])
+                nc.scalar.activation(yq[t][:, cols], q_ps[t][:, cols], ACT.Abs)
+            for t in range(NT):
+                mm(a_ps[t][:, cols], ca_w, ca_s, t, z_codes[:, cols], z_scales[:, cols])
+                nc.scalar.activation(sa[t][:, cols], a_ps[t][:, cols], ACT.Copy)
+
+        cb_w = gather_words("cb", l_cb, True, "z_bf1")
+        cb_s = gather_bytes("cb", l_cb, True, "planes1")
+
+        q_twin = four("q_twin", S)
+        dsum = four("dsum", S)
+        for t in range(NT):
+            nc.sync.dma_start(q_twin[t][:], yq[t][:, :S])
+        for t in range(NT):
+            nc.vector.tensor_tensor(dsum[t][:], yq[t][:].indirect(l_n6[:]), q_twin[t][:], ALU.add)
+
+        out_rows = out.rearrange("(u t b) j -> t u b j", t=NT, b=4)
+        g4, g3, low, twin = four("g4_", S), four("g3_", S), four("low", S), four("twin", S)
+        num, sq, inv, res = four("num", S), four("sq", S), four("inv", S), four("res", S)
+        mu = four("mu", 2 * S)
+
+        def front(t):
+            b_ps = bank(NT + t)
+            mm(b_ps[:], cb_w, cb_s, t, z_codes[:], z_scales[:])
+            nc.scalar.activation(g3[t][:], sa[t][:].indirect(l_n3[:]), ACT.Copy)
+            nc.scalar.activation(bg[t][:, :S], b_ps[:], ACT.Copy)
+            nc.scalar.activation(g4[t][:], bg[t][:].indirect(l_n4[:]), ACT.Copy)
+            nc.vector.tensor_tensor(low[t][:], b_ps[:], g3[t][:], ALU.min)
+            nc.vector.tensor_tensor(mu[t][:, S:], a_ps[t][:], g4[t][:], ALU.max)
+            nc.vector.tensor_tensor(mu[t][:, :S], low[t][:], mu[t][:, S:], ALU.subtract)
+            if t < NT - 1:
+                nc.sync.dma_start(twin[t][:], mu[t][:, :S])
+            else:
+                nc.vector.tensor_copy(twin[t][:], mu[t][:, :S])
+
+        def back(t):
+            nc.scalar.activation(sq[t][:], dsum[t][:], ACT.Square, bias=eight[:])
+            nc.scalar.activation(inv[t][:], sq[t][:], ACT.Abs_reciprocal_sqrt)
+            nc.vector.tensor_tensor(num[t][:], mu[t][:].indirect(l_n5[:]), twin[t][:], ALU.subtract)
+            nc.vector.tensor_tensor(res[t][:], num[t][:], inv[t][:], ALU.mult)
+            nc.sync.dma_start(out_rows[t], res[t][:])
+
+        for t in range(NT + 1):
+            if t < NT:
+                front(t)
+            if t > 0:
+                back(t - 1)

@@ -15,11 +15,15 @@ ACT = mybir.ActivationFunctionType
 P = 128
 T = 2048
 S = 512
-NT = 4
+PACK = 4
+TILES = S // P
+LAST = TILES - 1
 HALF = S // 2
-LCOLS = S // 16
+HALVES = (slice(0, HALF), slice(HALF, S))
+LIST_COLS = S // 16
+TWINS_ON_VECTOR = 2
 
-FLOPS = 4 * 2 * 512 * 512 * 512
+FLOPS = 4 * 2 * S * S * S
 
 
 def tile_picked_tricdmaxbnormbhop_none_p_kernel(
@@ -27,34 +31,43 @@ def tile_picked_tricdmaxbnormbhop_none_p_kernel(
 ):
     nc = tc.nc
     with ExitStack() as ctx:
-        keep = ctx.enter_context(tc.tile_pool(name="keep", bufs=1))
+        sbuf = ctx.enter_context(tc.tile_pool(name="sbuf", bufs=1))
         psum = ctx.enter_context(tc.psum_pool(name="psum", bufs=1))
 
-        def load_list(name, ap):
-            tl = keep.tile([P, LCOLS], U16, name="list_" + name)
-            nc.sync.dma_start(tl[:], ap)
-            return tl
+        def tile(name, shape, dtype, slot=None):
+            return sbuf.tile([P] + shape, dtype, name=name, tag=slot or name, align_bytes=64)
 
-        def four(name, width):
-            return [keep.tile([P, width], F32, name="%s%d" % (name, t)) for t in range(NT)]
+        def tiles(name, width):
+            return [tile("%s%d" % (name, t), [width], F32) for t in range(TILES)]
 
-        xs = keep.tile([P, T], U8, name="xs")
+        def bank(i):
+            return psum.tile([P, S], F32, name="bank%d" % i)
+
+        def load_list(name, src):
+            dst = sbuf.tile([P, LIST_COLS], U16, name="list_" + name)
+            nc.sync.dma_start(dst[:], src)
+            return dst
+
+        xs = tile("xs", [T], U8)
         nc.gpsimd.memset(xs[:].bitcast(I32), 0)
         l_offs = load_list("offs", offs)
-        for qd in range(4):
-            nc.scalar.dma_start(
-                xs[32 * qd : 32 * qd + 4, :].bitcast(I32),
-                x_scales[0, 4 * qd : 4 * qd + 4, :].bitcast(I32),
-            )
         l_cd = load_list("cd", cd)
-        w_raw = keep.tile([P, 4, S], F32, name="w_raw")
-        nc.sync.dma_start(w_raw[:], w1.rearrange("(p j) c -> p j c", j=4))
-        xw = keep.tile([P, T], I32, name="xw")
-        nc.sync.dma_start(xw[:], x_words[0].rearrange("p n t -> p (n t)").bitcast(I32))
-        gs_t = keep.tile([P, NT], F32, name="gs_t")
-        nc.gpsimd.dma_start(gs_t[:], gs.rearrange("(p t) o -> p (t o)", t=NT))
-        l_n1 = load_list("n1", n1)
+        for quad in range(4):
+            nc.sync.dma_start(
+                xs[32 * quad : 32 * quad + 4, :].bitcast(I32),
+                x_scales[0, 4 * quad : 4 * quad + 4, :].bitcast(I32),
+            )
         l_ca = load_list("ca", ca)
+        w_rows = w1.rearrange("(p j) c -> p j c", j=PACK)
+        w_raw = []
+        for h, cols in enumerate(HALVES):
+            w_raw.append(tile("w_raw%d" % h, [PACK, HALF], F32))
+            nc.sync.dma_start(w_raw[h][:], w_rows[:, :, cols])
+        xw = tile("xw", [T], I32)
+        nc.sync.dma_start(xw[:], x_words[0].rearrange("p n t -> p (n t)").bitcast(I32))
+        gs_t = tile("gs_t", [TILES], F32)
+        nc.gpsimd.dma_start(gs_t[:], gs.rearrange("(p t) o -> p (t o)", t=TILES))
+        l_n1 = load_list("n1", n1)
         l_n2 = load_list("n2", n2)
         l_cb = load_list("cb", cb)
         l_n6 = load_list("n6", n6)
@@ -62,140 +75,172 @@ def tile_picked_tricdmaxbnormbhop_none_p_kernel(
         l_n3 = load_list("n3", n3)
         l_n5 = load_list("n5", n5)
 
-        yq = four("yq", 2 * S)
-        for t in range(NT):
-            nc.gpsimd.memset(yq[t][:, S:], 0.0)
-        eight = keep.tile([P, 1], F32, name="eight")
-        nc.gpsimd.memset(eight[:], 8.0)
-        gs_half = keep.tile([P, NT], F32, name="gs_half")
-        nc.gpsimd.tensor_scalar(gs_half[:], gs_t[:], 0.5, 0.0, ALU.mult, ALU.add)
+        eight = tile("eight", [1], F32)
+        nc.vector.memset(eight[:], 8.0)
+        warm = tile("warm", [1], F32)
+        nc.scalar.activation(warm[:], eight[:], ACT.Abs_reciprocal_sqrt)
 
-        def gather_bytes(name, lst, dealt, tag):
-            got = keep.tile([P, S], U8, name="bytes_" + name, tag=tag, align_bytes=64)
+        win_yq = tiles("win_yq", 2 * S)
+        win_sa = tiles("win_sa", 2 * S)
+        win_b = tiles("win_b", 2 * S)
+        for win in win_yq + win_sa:
+            nc.vector.memset(win[:, S:], 0.0)
+        for win in win_b:
+            nc.gpsimd.memset(win[:, S:], 0.0)
+
+        gs_half = tile("gs_half", [TILES], F32)
+        nc.gpsimd.tensor_scalar(gs_half[:], gs_t[:], -0.5, 0.0, ALU.mult, ALU.add)
+        gs_neg = tile("gs_neg", [TILES], F32)
+        nc.gpsimd.tensor_scalar(gs_neg[:], gs_t[:], -1.0, 0.0, ALU.mult, ALU.add)
+
+        def pick_scales(name, lst, slot=None):
+            got = tile("scales_" + name, [S], U8, slot)
             nc.vector.tensor_copy(got[:], xs[:].indirect(lst[:]))
-            if not dealt:
-                return got
-            res = keep.tile([P, S], U8, name="dealt_" + name, align_bytes=64)
-            nc.vector.tensor_copy(
-                res[:].bitcast(I32).rearrange("p (t u) -> p t u", t=NT),
-                got[:].bitcast(I32).rearrange("p (u t) -> p t u", t=NT),
-            )
-            return res
-
-        def gather_words(name, lst, dealt, tag):
-            got = keep.tile([P, S], U32, name="words_" + name, tag=tag, align_bytes=64)
-            view = got[:].rearrange("p (t u b) -> p u t b", t=NT, b=4) if dealt else got[:]
-            nc.vector.tensor_copy(view, xw[:].bitcast(U32).indirect(lst[:]))
             return got
 
-        xq_s = gather_bytes("offs", l_offs, False, "xq_s")
-        cd_s = gather_bytes("cd", l_cd, True, "cd_s")
+        def pick_dealt_scales(name, lst, slot=None):
+            got = pick_scales(name, lst, slot)
+            dealt = tile("dealt_" + name, [S], U8)
+            nc.vector.tensor_copy(
+                dealt[:].bitcast(I32).rearrange("p (t u) -> p t u", t=TILES),
+                got[:].bitcast(I32).rearrange("p (u t) -> p t u", t=TILES),
+            )
+            return dealt
 
-        w_bf = keep.tile([P, NT * P * 4], BF16, name="w_bf", tag="w_bf", align_bytes=64)
-        nc.scalar.activation(
-            w_bf[:].rearrange("p (t m j) -> p m t j", t=NT, j=4),
-            w_raw[:].rearrange("p j (m t) -> p m t j", t=NT),
-            ACT.Copy,
-        )
-        xq_w = gather_words("offs", l_offs, False, "xq_w")
-        w_codes = keep.tile([P, S], U32, name="w_codes", tag="w_codes", align_bytes=64)
-        w_scales = keep.tile([P, S], U8, name="w_scales", tag="w_scales", align_bytes=64)
-        nc.vector.quantize_mx(out=w_codes[:].bitcast(FP8X4), scales=w_scales[:], in_=w_bf[:])
+        def pick_dealt_words(name, lst, slot=None):
+            got = tile("words_" + name, [S], U32, slot)
+            nc.vector.tensor_copy(
+                got[:].rearrange("p (t u e) -> p u t e", t=TILES, e=4),
+                xw[:].bitcast(U32).indirect(lst[:]),
+            )
+            return got
 
-        def bank(i):
-            return psum.tile([P, S], F32, name="bank%d" % i)
-
-        def mm(dst, words, scales, t, rw, rs):
+        def product(dst, words, scales, t, moving_words, moving_scales):
             cols = slice(t * P, (t + 1) * P)
             nc.tensor.matmul_mx(
-                out=dst, lhsT=words[:, cols].bitcast(FP8X4), lhsT_scale=scales[:, cols],
-                rhs=rw.bitcast(FP8X4), rhs_scale=rs, start=True, stop=True,
+                out=dst,
+                lhsT=words[:, cols].bitcast(FP8X4),
+                lhsT_scale=scales[:, cols],
+                rhs=moving_words.bitcast(FP8X4),
+                rhs_scale=moving_scales,
+                start=True,
+                stop=True,
             )
 
-        sa = four("sa", 2 * S)
-        for t in range(NT):
+        xq_scales = pick_scales("offs", l_offs)
+        cd_scales = pick_dealt_scales("cd", l_cd)
+        ca_scales = pick_dealt_scales("ca", l_ca)
+
+        w_bf = tile("w_bf", [S * PACK], BF16)
+        w_dealt = w_bf[:].rearrange("p (t m j) -> p m t j", t=TILES, j=PACK)
+        for h in range(2):
+            nc.scalar.activation(
+                w_dealt[:, h * P // 2 : (h + 1) * P // 2],
+                w_raw[h][:].rearrange("p j (m t) -> p m t j", t=TILES),
+                ACT.Copy,
+            )
+        w_words = tile("w_words", [S], U32)
+        w_scales = tile("w_scales", [S], U8)
+        nc.vector.quantize_mx(out=w_words[:].bitcast(FP8X4), scales=w_scales[:], in_=w_bf[:])
+        xq_words = tile("words_offs", [S], U32)
+        nc.vector.tensor_copy(xq_words[:], xw[:].bitcast(U32).indirect(l_offs[:]))
+
+        st_all = tile("st_all", [TILES, S], F32)
+        for t in range(TILES):
             y_ps = bank(t)
-            mm(y_ps[:], w_codes, w_scales, t, xq_w[:], xq_s[:])
-            nc.scalar.activation(yq[t][:, :S], y_ps[:], ACT.Copy, scale=gs_half[:, t : t + 1])
-            nc.scalar.activation(sa[t][:, S:], yq[t][:].indirect(l_n1[:]), ACT.Copy)
-            nc.vector.scalar_tensor_tensor(
-                sa[t][:, :S], y_ps[:], gs_t[:, t : t + 1], sa[t][:, S:], ALU.mult, ALU.add
-            )
-
-        cd_w = gather_words("cd", l_cd, True, "w_bf")
-        ca_w = gather_words("ca", l_ca, True, "w_codes")
-        ca_s = gather_bytes("ca", l_ca, True, "w_scales")
-
-        bg = four("bg", 2 * S)
-        z_codes = keep.tile([P, S], U32, name="z_codes", align_bytes=64)
-        z_scales = keep.tile([P, S], U8, name="z_scales", align_bytes=64)
-        q_ps = [bank(NT + t) for t in range(NT)]
-        a_ps = [bank(t) for t in range(NT)]
-        for h in range(2):
-            for t in range(NT):
-                nc.scalar.activation(
-                    bg[t][:, S + h * HALF : S + (h + 1) * HALF],
-                    sa[t][:].indirect(l_n2[:, h * LCOLS // 2 : (h + 1) * LCOLS // 2]),
-                    ACT.Copy,
-                )
-        for h in range(2):
-            cols = slice(h * HALF, (h + 1) * HALF)
-            planes = keep.tile([P, NT, HALF], BF16, name="planes%d" % h, tag="planes%d" % h, align_bytes=64)
-            for t in range(NT):
-                nc.vector.tensor_tensor(
-                    planes[:, t, :], sa[t][:, cols], bg[t][:, S + h * HALF : S + (h + 1) * HALF], ALU.subtract
-                )
-            z_bf = keep.tile([P, HALF * 4], BF16, name="z_bf%d" % h, tag="z_bf%d" % h, align_bytes=64)
-            nc.vector.tensor_copy(
-                z_bf[:].rearrange("p (c i t) -> p c t i", i=4, t=NT),
-                planes[:].rearrange("p t (c i) -> p c t i", i=4),
-            )
-            nc.vector.quantize_mx(out=z_codes[:, cols].bitcast(FP8X4), scales=z_scales[:, cols], in_=z_bf[:])
-            for t in range(NT):
-                mm(q_ps[t][:, cols], cd_w, cd_s, t, z_codes[:, cols], z_scales[:, cols])
-                nc.scalar.activation(yq[t][:, cols], q_ps[t][:, cols], ACT.Abs)
-            for t in range(NT):
-                mm(a_ps[t][:, cols], ca_w, ca_s, t, z_codes[:, cols], z_scales[:, cols])
-                nc.scalar.activation(sa[t][:, cols], a_ps[t][:, cols], ACT.Copy)
-
-        cb_w = gather_words("cb", l_cb, True, "z_bf1")
-        cb_s = gather_bytes("cb", l_cb, True, "planes1")
-
-        q_twin = four("q_twin", S)
-        dsum = four("dsum", S)
-        for t in range(NT):
-            nc.sync.dma_start(q_twin[t][:], yq[t][:, :S])
-        for t in range(NT):
-            nc.vector.tensor_tensor(dsum[t][:], yq[t][:].indirect(l_n6[:]), q_twin[t][:], ALU.add)
-
-        out_rows = out.rearrange("(u t b) j -> t u b j", t=NT, b=4)
-        g4, g3, low, twin = four("g4_", S), four("g3_", S), four("low", S), four("twin", S)
-        num, sq, inv, res = four("num", S), four("sq", S), four("inv", S), four("res", S)
-        mu = four("mu", 2 * S)
-
-        def front(t):
-            b_ps = bank(NT + t)
-            mm(b_ps[:], cb_w, cb_s, t, z_codes[:], z_scales[:])
-            nc.scalar.activation(g3[t][:], sa[t][:].indirect(l_n3[:]), ACT.Copy)
-            nc.scalar.activation(bg[t][:, :S], b_ps[:], ACT.Copy)
-            nc.scalar.activation(g4[t][:], bg[t][:].indirect(l_n4[:]), ACT.Copy)
-            nc.vector.tensor_tensor(low[t][:], b_ps[:], g3[t][:], ALU.min)
-            nc.vector.tensor_tensor(mu[t][:, S:], a_ps[t][:], g4[t][:], ALU.max)
-            nc.vector.tensor_tensor(mu[t][:, :S], low[t][:], mu[t][:, S:], ALU.subtract)
-            if t < NT - 1:
-                nc.sync.dma_start(twin[t][:], mu[t][:, :S])
+            y_plain = tile("y_plain%d" % t, [S], F32)
+            product(y_ps[:], w_words, w_scales, t, xq_words[:], xq_scales[:])
+            nc.scalar.activation(win_yq[t][:, :S], y_ps[:], ACT.Copy, scale=gs_half[:, t : t + 1])
+            nc.scalar.activation(y_plain[:], y_ps[:], ACT.Copy, scale=gs_neg[:, t : t + 1])
+            nc.vector.tensor_tensor(win_sa[t][:, :S], win_yq[t][:].indirect(l_n1[:]), y_plain[:], ALU.add)
+            if t < LAST:
+                nc.sync.dma_start(st_all[:, t, :], win_sa[t][:, :S])
             else:
-                nc.vector.tensor_copy(twin[t][:], mu[t][:, :S])
+                nc.vector.tensor_copy(st_all[:, t, :], win_sa[t][:, :S])
 
-        def back(t):
-            nc.scalar.activation(sq[t][:], dsum[t][:], ACT.Square, bias=eight[:])
-            nc.scalar.activation(inv[t][:], sq[t][:], ACT.Abs_reciprocal_sqrt)
-            nc.vector.tensor_tensor(num[t][:], mu[t][:].indirect(l_n5[:]), twin[t][:], ALU.subtract)
-            nc.vector.tensor_tensor(res[t][:], num[t][:], inv[t][:], ALU.mult)
-            nc.sync.dma_start(out_rows[t], res[t][:])
+        cd_words = pick_dealt_words("cd", l_cd)
+        ca_words = pick_dealt_words("ca", l_ca)
+        cb_scales = pick_dealt_scales("cb", l_cb, slot="y_plain%d" % LAST)
 
-        for t in range(NT + 1):
-            if t < NT:
-                front(t)
+        st_n2 = tile("st_n2", [TILES, S], F32)
+        z_words = tile("z_words", [S], U32)
+        z_scales = tile("z_scales", [S], U8)
+        q_ps = [bank(TILES + t) for t in range(TILES)]
+        a_ps = [bank(t) for t in range(TILES)]
+        for h, cols in enumerate(HALVES):
+            entries = l_n2[:, h * LIST_COLS // 2 : (h + 1) * LIST_COLS // 2]
+            for t in range(TILES):
+                nc.scalar.activation(st_n2[:, t, cols], win_sa[t][:].indirect(entries), ACT.Copy)
+        for h, cols in enumerate(HALVES):
+            z_bf = tile("z_bf%d" % h, [HALF * PACK], BF16, slot="z_bf")
+            nc.vector.tensor_tensor(
+                z_bf[:].rearrange("p (c i t) -> p c t i", i=4, t=TILES),
+                st_n2[:, :, cols].rearrange("p t (c i) -> p c t i", i=4),
+                st_all[:, :, cols].rearrange("p t (c i) -> p c t i", i=4),
+                ALU.subtract,
+            )
+            nc.vector.quantize_mx(out=z_words[:, cols].bitcast(FP8X4), scales=z_scales[:, cols], in_=z_bf[:])
+            for t in range(TILES):
+                product(q_ps[t][:, cols], cd_words, cd_scales, t, z_words[:, cols], z_scales[:, cols])
+                nc.scalar.activation(win_yq[t][:, cols], q_ps[t][:, cols], ACT.Abs)
+            product(a_ps[0][:, cols], ca_words, ca_scales, 0, z_words[:, cols], z_scales[:, cols])
+            nc.scalar.activation(win_sa[0][:, cols], a_ps[0][:, cols], ACT.Copy)
+
+        cb_words = pick_dealt_words("cb", l_cb, slot="z_bf")
+
+        q_twin = tiles("q_twin", S)
+        q_sum = tiles("q_sum", S)
+        for t in range(TILES):
+            if t < TWINS_ON_VECTOR:
+                nc.vector.tensor_copy(q_twin[t][:], win_yq[t][:, :S])
+            else:
+                nc.sync.dma_start(q_twin[t][:], win_yq[t][:, :S])
+            nc.vector.tensor_tensor(q_sum[t][:], win_yq[t][:].indirect(l_n6[:]), q_twin[t][:], ALU.add)
+
+        a_n3 = tiles("a_n3_", S)
+        b_n4 = tiles("b_n4_", S)
+        m_twin = tiles("m_twin", S)
+        low_slots = ("q_twin2", "b_n4_0", "m_twin0", "m_twin1")
+        win_m_slots = ("q_twin3", "q_twin2")
+        win_m = []
+        numer = []
+
+        def spread(t):
+            b_ps = bank(TILES + t)
             if t > 0:
-                back(t - 1)
+                product(a_ps[t][:], ca_words, ca_scales, t, z_words[:], z_scales[:])
+                nc.scalar.activation(win_sa[t][:, :S], a_ps[t][:], ACT.Copy)
+            product(b_ps[:], cb_words, cb_scales, t, z_words[:], z_scales[:])
+            nc.scalar.activation(a_n3[t][:], win_sa[t][:].indirect(l_n3[:]), ACT.Copy)
+            nc.scalar.activation(win_b[t][:, :S], b_ps[:], ACT.Copy)
+            nc.scalar.activation(b_n4[t][:], win_b[t][:].indirect(l_n4[:]), ACT.Copy)
+            low = tile("low%d" % t, [S], F32, slot=low_slots[t])
+            nc.vector.tensor_tensor(low[:], b_ps[:], a_n3[t][:], ALU.min)
+            win = tile("win_m%d" % t, [2 * S], F32, slot=win_m_slots[t % 2])
+            nc.vector.tensor_tensor(win[:, S:], a_ps[t][:], b_n4[t][:], ALU.max)
+            nc.vector.tensor_tensor(win[:, :S], low[:], win[:, S:], ALU.subtract)
+            if t < LAST:
+                nc.sync.dma_start(m_twin[t][:], win[:, :S])
+            else:
+                nc.vector.tensor_copy(m_twin[t][:], win[:, :S])
+            win_m.append(win)
+
+        def numerator(t):
+            numer.append(tile("numer%d" % t, [S], F32))
+            nc.vector.tensor_tensor(numer[t][:], win_m[t][:].indirect(l_n5[:]), m_twin[t][:], ALU.subtract)
+
+        for t in range(TILES):
+            spread(t)
+            if t > 0:
+                numerator(t - 1)
+        numerator(LAST)
+
+        out_rows = out.rearrange("(u t e) j -> t u e j", t=TILES, e=4)
+        for t in range(TILES):
+            inv_root = tile("inv_root%d" % t, [S], F32)
+            nc.scalar.activation(inv_root[:], q_sum[t][:], ACT.Abs_reciprocal_sqrt, bias=eight[:])
+            inverse = tile("inverse%d" % t, [S], F32)
+            nc.scalar.activation(inverse[:], inv_root[:], ACT.Square)
+            result = tile("result%d" % t, [S], F32, slot="m_twin%d" % (t + 1) if t < LAST else None)
+            nc.vector.tensor_tensor(result[:], numer[t][:], inverse[:], ALU.mult)
+            nc.sync.dma_start(out_rows[t], result[:])

from contextlib import ExitStack

import concourse.mybir as mybir

F32 = mybir.dt.float32
BF16 = mybir.dt.bfloat16
I32 = mybir.dt.int32
U32 = mybir.dt.uint32
U16 = mybir.dt.uint16
U8 = mybir.dt.uint8
FP8X4 = mybir.dt.float8_e4m3fn_x4
ALU = mybir.AluOpType
ACT = mybir.ActivationFunctionType

P = 128
T = 2048
S = 512
PACK = 4
TILES = S // P
LAST = TILES - 1
HALF = S // 2
HALVES = (slice(0, HALF), slice(HALF, S))
LIST_COLS = S // 16
TWINS_ON_VECTOR = 2

FLOPS = 4 * 2 * S * S * S


def tile_picked_tricdmaxbnormbhop_none_p_kernel(
    tc, x_words, x_scales, w1, gs, offs, n1, n2, ca, cb, cd, n3, n4, n5, n6, out
):
    nc = tc.nc
    with ExitStack() as ctx:
        sbuf = ctx.enter_context(tc.tile_pool(name="sbuf", bufs=1))
        psum = ctx.enter_context(tc.psum_pool(name="psum", bufs=1))

        def tile(name, shape, dtype, slot=None):
            return sbuf.tile([P] + shape, dtype, name=name, tag=slot or name, align_bytes=64)

        def tiles(name, width):
            return [tile("%s%d" % (name, t), [width], F32) for t in range(TILES)]

        def bank(i):
            return psum.tile([P, S], F32, name="bank%d" % i)

        def load_list(name, src):
            dst = sbuf.tile([P, LIST_COLS], U16, name="list_" + name)
            nc.sync.dma_start(dst[:], src)
            return dst

        xs = tile("xs", [T], U8)
        nc.gpsimd.memset(xs[:].bitcast(I32), 0)
        l_offs = load_list("offs", offs)
        l_cd = load_list("cd", cd)
        for quad in range(4):
            nc.sync.dma_start(
                xs[32 * quad : 32 * quad + 4, :].bitcast(I32),
                x_scales[0, 4 * quad : 4 * quad + 4, :].bitcast(I32),
            )
        l_ca = load_list("ca", ca)
        w_rows = w1.rearrange("(p j) c -> p j c", j=PACK)
        w_raw = []
        for h, cols in enumerate(HALVES):
            w_raw.append(tile("w_raw%d" % h, [PACK, HALF], F32))
            nc.sync.dma_start(w_raw[h][:], w_rows[:, :, cols])
        xw = tile("xw", [T], I32)
        nc.sync.dma_start(xw[:], x_words[0].rearrange("p n t -> p (n t)").bitcast(I32))
        gs_t = tile("gs_t", [TILES], F32)
        nc.gpsimd.dma_start(gs_t[:], gs.rearrange("(p t) o -> p (t o)", t=TILES))
        l_n1 = load_list("n1", n1)
        l_n2 = load_list("n2", n2)
        l_cb = load_list("cb", cb)
        l_n6 = load_list("n6", n6)
        l_n4 = load_list("n4", n4)
        l_n3 = load_list("n3", n3)
        l_n5 = load_list("n5", n5)

        eight = tile("eight", [1], F32)
        nc.vector.memset(eight[:], 8.0)
        warm = tile("warm", [1], F32)
        nc.scalar.activation(warm[:], eight[:], ACT.Abs_reciprocal_sqrt)

        win_yq = tiles("win_yq", 2 * S)
        win_sa = tiles("win_sa", 2 * S)
        win_b = tiles("win_b", 2 * S)
        for win in win_yq + win_sa:
            nc.vector.memset(win[:, S:], 0.0)
        for win in win_b:
            nc.gpsimd.memset(win[:, S:], 0.0)

        gs_half = tile("gs_half", [TILES], F32)
        nc.gpsimd.tensor_scalar(gs_half[:], gs_t[:], -0.5, 0.0, ALU.mult, ALU.add)
        gs_neg = tile("gs_neg", [TILES], F32)
        nc.gpsimd.tensor_scalar(gs_neg[:], gs_t[:], -1.0, 0.0, ALU.mult, ALU.add)

        def pick_scales(name, lst, slot=None):
            got = tile("scales_" + name, [S], U8, slot)
            nc.vector.tensor_copy(got[:], xs[:].indirect(lst[:]))
            return got

        def pick_dealt_scales(name, lst, slot=None):
            got = pick_scales(name, lst, slot)
            dealt = tile("dealt_" + name, [S], U8)
            nc.vector.tensor_copy(
                dealt[:].bitcast(I32).rearrange("p (t u) -> p t u", t=TILES),
                got[:].bitcast(I32).rearrange("p (u t) -> p t u", t=TILES),
            )
            return dealt

        def pick_dealt_words(name, lst, slot=None):
            got = tile("words_" + name, [S], U32, slot)
            nc.vector.tensor_copy(
                got[:].rearrange("p (t u e) -> p u t e", t=TILES, e=4),
                xw[:].bitcast(U32).indirect(lst[:]),
            )
            return got

        def product(dst, words, scales, t, moving_words, moving_scales):
            cols = slice(t * P, (t + 1) * P)
            nc.tensor.matmul_mx(
                out=dst,
                lhsT=words[:, cols].bitcast(FP8X4),
                lhsT_scale=scales[:, cols],
                rhs=moving_words.bitcast(FP8X4),
                rhs_scale=moving_scales,
                start=True,
                stop=True,
            )

        xq_scales = pick_scales("offs", l_offs)
        cd_scales = pick_dealt_scales("cd", l_cd)
        ca_scales = pick_dealt_scales("ca", l_ca)

        w_bf = tile("w_bf", [S * PACK], BF16)
        w_dealt = w_bf[:].rearrange("p (t m j) -> p m t j", t=TILES, j=PACK)
        for h in range(2):
            nc.scalar.activation(
                w_dealt[:, h * P // 2 : (h + 1) * P // 2],
                w_raw[h][:].rearrange("p j (m t) -> p m t j", t=TILES),
                ACT.Copy,
            )
        w_words = tile("w_words", [S], U32)
        w_scales = tile("w_scales", [S], U8)
        nc.vector.quantize_mx(out=w_words[:].bitcast(FP8X4), scales=w_scales[:], in_=w_bf[:])
        xq_words = tile("words_offs", [S], U32)
        nc.vector.tensor_copy(xq_words[:], xw[:].bitcast(U32).indirect(l_offs[:]))

        st_all = tile("st_all", [TILES, S], F32)
        for t in range(TILES):
            y_ps = bank(t)
            y_plain = tile("y_plain%d" % t, [S], F32)
            product(y_ps[:], w_words, w_scales, t, xq_words[:], xq_scales[:])
            nc.scalar.activation(win_yq[t][:, :S], y_ps[:], ACT.Copy, scale=gs_half[:, t : t + 1])
            nc.scalar.activation(y_plain[:], y_ps[:], ACT.Copy, scale=gs_neg[:, t : t + 1])
            nc.vector.tensor_tensor(win_sa[t][:, :S], win_yq[t][:].indirect(l_n1[:]), y_plain[:], ALU.add)
            if t < LAST:
                nc.sync.dma_start(st_all[:, t, :], win_sa[t][:, :S])
            else:
                nc.vector.tensor_copy(st_all[:, t, :], win_sa[t][:, :S])

        cd_words = pick_dealt_words("cd", l_cd)
        ca_words = pick_dealt_words("ca", l_ca)
        cb_scales = pick_dealt_scales("cb", l_cb, slot="y_plain%d" % LAST)

        st_n2 = tile("st_n2", [TILES, S], F32)
        z_words = tile("z_words", [S], U32)
        z_scales = tile("z_scales", [S], U8)
        q_ps = [bank(TILES + t) for t in range(TILES)]
        a_ps = [bank(t) for t in range(TILES)]
        for h, cols in enumerate(HALVES):
            entries = l_n2[:, h * LIST_COLS // 2 : (h + 1) * LIST_COLS // 2]
            for t in range(TILES):
                nc.scalar.activation(st_n2[:, t, cols], win_sa[t][:].indirect(entries), ACT.Copy)
        for h, cols in enumerate(HALVES):
            z_bf = tile("z_bf%d" % h, [HALF * PACK], BF16, slot="z_bf")
            nc.vector.tensor_tensor(
                z_bf[:].rearrange("p (c i t) -> p c t i", i=4, t=TILES),
                st_n2[:, :, cols].rearrange("p t (c i) -> p c t i", i=4),
                st_all[:, :, cols].rearrange("p t (c i) -> p c t i", i=4),
                ALU.subtract,
            )
            nc.vector.quantize_mx(out=z_words[:, cols].bitcast(FP8X4), scales=z_scales[:, cols], in_=z_bf[:])
            for t in range(TILES):
                product(q_ps[t][:, cols], cd_words, cd_scales, t, z_words[:, cols], z_scales[:, cols])
                nc.scalar.activation(win_yq[t][:, cols], q_ps[t][:, cols], ACT.Abs)
            product(a_ps[0][:, cols], ca_words, ca_scales, 0, z_words[:, cols], z_scales[:, cols])
            nc.scalar.activation(win_sa[0][:, cols], a_ps[0][:, cols], ACT.Copy)

        cb_words = pick_dealt_words("cb", l_cb, slot="z_bf")

        q_twin = tiles("q_twin", S)
        q_sum = tiles("q_sum", S)
        for t in range(TILES):
            if t < TWINS_ON_VECTOR:
                nc.vector.tensor_copy(q_twin[t][:], win_yq[t][:, :S])
            else:
                nc.sync.dma_start(q_twin[t][:], win_yq[t][:, :S])
            nc.vector.tensor_tensor(q_sum[t][:], win_yq[t][:].indirect(l_n6[:]), q_twin[t][:], ALU.add)

        a_n3 = tiles("a_n3_", S)
        b_n4 = tiles("b_n4_", S)
        m_twin = tiles("m_twin", S)
        low_slots = ("q_twin2", "b_n4_0", "m_twin0", "m_twin1")
        win_m_slots = ("q_twin3", "q_twin2")
        win_m = []
        numer = []

        def spread(t):
            b_ps = bank(TILES + t)
            if t > 0:
                product(a_ps[t][:], ca_words, ca_scales, t, z_words[:], z_scales[:])
                nc.scalar.activation(win_sa[t][:, :S], a_ps[t][:], ACT.Copy)
            product(b_ps[:], cb_words, cb_scales, t, z_words[:], z_scales[:])
            nc.scalar.activation(a_n3[t][:], win_sa[t][:].indirect(l_n3[:]), ACT.Copy)
            nc.scalar.activation(win_b[t][:, :S], b_ps[:], ACT.Copy)
            nc.scalar.activation(b_n4[t][:], win_b[t][:].indirect(l_n4[:]), ACT.Copy)
            low = tile("low%d" % t, [S], F32, slot=low_slots[t])
            nc.vector.tensor_tensor(low[:], b_ps[:], a_n3[t][:], ALU.min)
            win = tile("win_m%d" % t, [2 * S], F32, slot=win_m_slots[t % 2])
            nc.vector.tensor_tensor(win[:, S:], a_ps[t][:], b_n4[t][:], ALU.max)
            nc.vector.tensor_tensor(win[:, :S], low[:], win[:, S:], ALU.subtract)
            if t < LAST:
                nc.sync.dma_start(m_twin[t][:], win[:, :S])
            else:
                nc.vector.tensor_copy(m_twin[t][:], win[:, :S])
            win_m.append(win)

        def numerator(t):
            numer.append(tile("numer%d" % t, [S], F32))
            nc.vector.tensor_tensor(numer[t][:], win_m[t][:].indirect(l_n5[:]), m_twin[t][:], ALU.subtract)

        for t in range(TILES):
            spread(t)
            if t > 0:
                numerator(t - 1)
        numerator(LAST)

        out_rows = out.rearrange("(u t e) j -> t u e j", t=TILES, e=4)
        for t in range(TILES):
            inv_root = tile("inv_root%d" % t, [S], F32)
            nc.scalar.activation(inv_root[:], q_sum[t][:], ACT.Abs_reciprocal_sqrt, bias=eight[:])
            inverse = tile("inverse%d" % t, [S], F32)
            nc.scalar.activation(inverse[:], inv_root[:], ACT.Square)
            result = tile("result%d" % t, [S], F32, slot="m_twin%d" % (t + 1) if t < LAST else None)
            nc.vector.tensor_tensor(result[:], numer[t][:], inverse[:], ALU.mult)
            nc.sync.dma_start(out_rows[t], result[:])
